import numpy as np
import ml_dtypes


def mxq(x, axis, fmt="e4m3"):
    dtype, down = {"e4m3": (ml_dtypes.float8_e4m3fn, 7), "e5m2": (ml_dtypes.float8_e5m2, 14)}[fmt]
    v = np.moveaxis(np.asarray(x, np.float32).astype(ml_dtypes.bfloat16).astype(np.float64), axis, -1)
    blocks = v.reshape(v.shape[:-1] + (-1, 32))
    amax = np.abs(blocks).max(-1, keepdims=True)
    byte = np.maximum(np.where(amax > 0, np.frexp(amax)[1] - 1 + 127, 0) - down, 1)
    scale = np.exp2(byte - 127.0)
    codes = (blocks / scale).astype(np.float32).astype(dtype).astype(np.float64)
    return np.moveaxis((codes * scale).reshape(v.shape), -1, axis)


WIDE = False


def mx_kscale(k):
    if not WIDE:
        return np.ones(k)
    levels = np.array([10, -10, 5, -5, 0])
    if k % 512:
        return np.exp2(np.random.permutation(np.resize(levels, k // 32))).repeat(32)
    a = np.empty((k // 512, 16))
    for p in range(k // 512):
        a[p, :8] = np.random.permutation(np.resize(levels, 8))
        for g in range(8):
            far = levels[np.abs(levels - a[p, g]) >= 10]
            a[p, g + 8] = far[np.random.randint(len(far))]
    return np.exp2(a.ravel()).repeat(32)


def f64(x):
    return np.asarray(x).astype(np.float64)


def striped(idx):
    return np.tile(idx.reshape(-1, 16).T, (8, 1)).astype(np.uint16)


def unstriped(offs):
    return offs[:16].T.reshape(-1).astype(np.int64)


def striped8(idx):
    return np.concatenate([x.reshape(-1, 16).T for x in idx]).astype(np.uint16)


def runs(offs, k):
    lists = np.stack([offs[16 * r : 16 * r + 16].T.reshape(-1) for r in range(8)]).astype(np.int64)
    return lists[np.arange(k) % 512 // 64]


def pack_weight(w):
    k, n = w.shape
    w = f64(np.asarray(w, np.float32).astype(ml_dtypes.bfloat16)).reshape(k // 32, 32, n)
    amax = np.abs(w).max(1)
    byte = np.clip(np.where(amax > 0, np.frexp(amax)[1] - 1 + 127 - 7, 1), 1, 254)
    scaled = (w * np.exp2(127.0 - byte)[:, None, :]).reshape(k, n).astype(np.float32)
    words = np.ascontiguousarray(scaled.reshape(k // 512, 128, 4, n).transpose(0, 1, 3, 2)).astype(ml_dtypes.float8_e4m3fn).view(np.uint8)
    return words, np.ascontiguousarray(byte.astype(np.uint8).reshape(k // 512, 16, n))


def unpack_weight(words, scales):
    g, p, n, _ = words.shape
    vals = np.ascontiguousarray(words).view(ml_dtypes.float8_e4m3fn).astype(np.float64) * np.repeat(np.exp2(scales.astype(np.float64) - 127.0), 8, axis=1)[..., None]
    return vals.transpose(0, 1, 3, 2).reshape(g * 512, n)


K, T, S, V, N, H, W = 512, 2048, 1024, 512, 512, 512, 256


def setup_inputs():
    n = np.random.standard_normal
    s = mx_kscale(K)[:, None]
    u = mx_kscale(H)
    packed_xT = pack_weight(n((K, T)) * s)
    perm = np.stack([np.random.permutation(V) for _ in range(8)])
    return {
        "x_words": packed_xT[0],
        "x_scales": packed_xT[1],
        "w1": (n((K, H)) / np.sqrt(K) / s * u).astype(np.float32),
        "w2": (n((H, H)) / np.sqrt(H) / u[:, None] * u).astype(np.float32),
        "w3": (n((H, N)) / np.sqrt(H) / u[:, None]).astype(np.float32),
        "res": n((N, V)).astype(np.float32),
        "offs": striped(np.random.permutation(T)[:S]),
        "n1": striped8(np.stack([np.random.permutation(S) for _ in range(8)])),
        "n2": striped8(perm[:, :W]),
        "n3": striped8(perm[:, W:]),
    }


def reference(x_words, x_scales, w1, w2, w3, res, offs, n1, n2, n3):
    xq = unpack_weight(x_words, x_scales)[:, unstriped(offs)]
    y = mxq(f64(w1), 0, "e4m3").T @ xq
    ln = y[np.arange(H)[:, None], runs(n1, H)]
    mx = ln.reshape(H, V, 2).max(axis=2)
    mn = ln.reshape(H, V, 2).min(axis=2)
    z = mx - (0.5 * mn)
    h = mxq(f64(w2), 0, "e4m3").T @ mxq(z, 0, "e4m3")
    pa = h[np.arange(H)[:, None], runs(n2, H)]
    pb = h[np.arange(H)[:, None], runs(n3, H)]
    rb = np.minimum(pa, pb)
    ra = np.maximum(pa, pb)
    ds = np.zeros((H, V))
    ds[np.arange(H)[:, None], runs(n2, H)] = ra
    z2 = ds.copy()
    z2[np.arange(H)[:, None], runs(n3, H)] = rb
    return f64(res) + (mxq(f64(w3), 0, "e4m3").T @ mxq(z2, 0, "e4m3"))

@@ -1,0 +1,182 @@
+from contextlib import ExitStack
+
+import concourse.mybir as mybir
+
+K, T, S, V, N, H, W = 512, 2048, 1024, 512, 512, 512, 256
+FLOPS = 2 * K * H * S + 2 * H * H * V + 2 * H * N * V
+
+F32 = mybir.dt.float32
+BF16 = mybir.dt.bfloat16
+I32 = mybir.dt.int32
+U32 = mybir.dt.uint32
+U16 = mybir.dt.uint16
+U8 = mybir.dt.uint8
+X4 = mybir.dt.float8_e4m3fn_x4
+ALU = mybir.AluOpType
+
+P = 128
+SLOTS = 4
+RUN = 4
+BANK = 512
+Z_CHUNKS = [(0, 256), (256, 128), (384, 128)]
+OUT_CHUNK = 128
+
+
+def tile_picked_deeppgaporder_none_p_kernel(tc, x_words, x_scales, w1, w2, w3, res, offs, n1, n2, n3, out):
+    nc = tc.nc
+    with ExitStack() as ctx:
+        keep = ctx.enter_context(tc.tile_pool(name="keep", bufs=1))
+        psum = ctx.enter_context(tc.psum_pool(name="psum", bufs=1))
+
+        def sb(name, shape, dtype):
+            return keep.tile(shape, dtype, name=name, align_bytes=64)
+
+        def bank(i):
+            return psum.tile([P, BANK], F32, name="bank%d" % i)
+
+        offs_t = sb("offs_t", [P, S // 16], U16)
+        n1_t = sb("n1_t", [P, S // 16], U16)
+        n2_t = sb("n2_t", [P, W // 16], U16)
+        n3_t = sb("n3_t", [P, W // 16], U16)
+        xs_all = sb("xs_all", [P, T], U8)
+        xw_all = sb("xw_all", [P, T], I32)
+        nc.vector.memset(xs_all[:].bitcast(I32), 0)
+        nc.sync.dma_start(offs_t[:], offs)
+        for q in range(4):
+            nc.sync.dma_start(xs_all[32 * q : 32 * q + 4, :].bitcast(I32), x_scales[0, 4 * q : 4 * q + 4, :].bitcast(I32))
+        nc.sync.dma_start(xw_all[:], x_words[0].rearrange("p c r -> p (c r)").bitcast(I32))
+        w1_raw = sb("w1_raw", [P, SLOTS, H], F32)
+        nc.sync.dma_start(w1_raw[:], w1.rearrange("(p j) h -> p j h", j=SLOTS))
+        nc.sync.dma_start(n1_t[:], n1)
+
+        def load_dealt_rows(name, w):
+            raw = sb(name, [P, SLOTS, w.shape[1]], F32)
+            rows = w.rearrange("(a t q) n -> t a q n", t=SLOTS, q=RUN)
+            for t in range(SLOTS):
+                nc.sync.dma_start(raw[:, t, :], rows[t])
+            return raw
+
+        w2_raw = load_dealt_rows("w2_raw", w2)
+        nc.sync.dma_start(n2_t[:], n2)
+        nc.sync.dma_start(n3_t[:], n3)
+        w3_raw = load_dealt_rows("w3_raw", w3)
+        res_t = sb("res_t", [P, N // P, V], F32)
+        nc.sync.dma_start(res_t[:], res.rearrange("(t p) v -> p t v", p=P))
+
+        xs = sb("xs", [P, S], U8)
+        xw = sb("xw", [P, S], U32)
+        nc.vector.tensor_copy(xs[:], xs_all[:].indirect(offs_t[:]))
+        nc.vector.tensor_copy(xw[:], xw_all[:].bitcast(U32).indirect(offs_t[:]))
+
+        def deal_columns(copy, dst, raw, t):
+            copy(
+                dst.rearrange("p (a q j) -> p a j q", q=RUN, j=SLOTS),
+                raw[:].rearrange("p j (a t q) -> p t a j q", t=SLOTS, q=RUN)[:, t],
+            )
+
+        w1_codes = sb("w1_codes", [P, H], U32)
+        w1_scales = sb("w1_scales", [P, H], U8)
+        w1_bf = [sb("w1_bf%d" % t, [P, P * SLOTS], BF16) for t in range(SLOTS)]
+        y = [sb("y%d" % t, [P, S], F32) for t in range(SLOTS)]
+        for t in range(SLOTS):
+            deal_columns(nc.scalar.copy if t < 2 else nc.vector.tensor_copy, w1_bf[t][:], w1_raw, t)
+        for t in range(SLOTS):
+            cols = slice(t * P, (t + 1) * P)
+            nc.vector.quantize_mx(out=w1_codes[:, cols].bitcast(X4), scales=w1_scales[:, cols], in_=w1_bf[t][:])
+        for t in range(SLOTS):
+            cols = slice(t * P, (t + 1) * P)
+            for half in range(S // BANK):
+                tok = slice(half * BANK, (half + 1) * BANK)
+                acc = bank((2 * t + half) % 4)
+                nc.tensor.matmul_mx(
+                    out=acc[:], lhsT=w1_codes[:, cols].bitcast(X4), lhsT_scale=w1_scales[:, cols],
+                    rhs=xw[:, tok].bitcast(X4), rhs_scale=xs[:, tok], start=True, stop=True,
+                )
+                nc.scalar.copy(y[t][:, tok], acc[:])
+
+        w2_codes = sb("w2_codes", [P, H], U32)
+        w2_scales = sb("w2_scales", [P, H], U8)
+        w2_bf = sb("w2_bf", [P, H * SLOTS], BF16)
+        for t in range(SLOTS):
+            deal_columns(nc.scalar.copy, w2_bf[:, t * BANK : (t + 1) * BANK], w2_raw, t)
+        nc.vector.quantize_mx(out=w2_codes[:].bitcast(X4), scales=w2_scales[:], in_=w2_bf[:])
+
+        h = [sb("h%d" % t, [P, V], F32) for t in range(SLOTS)]
+        h_acc = [bank(4 + t) for t in range(SLOTS)]
+        for c, (v0, nv) in enumerate(Z_CHUNKS):
+            first = sb("first%d" % c, [P, SLOTS, nv], F32)
+            second = sb("second%d" % c, [P, SLOTS, nv], F32)
+            lined = []
+            for t in range(SLOTS + 1):
+                if t < SLOTS:
+                    ln = sb("ln%d_%d" % (c, t), [P, 2 * nv], F32)
+                    nc.vector.tensor_copy(ln[:], y[t][:].indirect(n1_t[:, v0 // 8 : (v0 + nv) // 8]))
+                    lined.append(ln)
+                if t > 0:
+                    pair = lined[t - 1][:].rearrange("p (v e) -> p e v", e=2)
+                    nc.vector.scalar_tensor_tensor(first[:, t - 1, :], pair[:, 1], -0.5, pair[:, 0], ALU.mult, ALU.add)
+                    nc.vector.scalar_tensor_tensor(second[:, t - 1, :], pair[:, 0], -0.5, pair[:, 1], ALU.mult, ALU.add)
+            z_bf = sb("z_bf%d" % c, [P, nv * SLOTS], BF16)
+            nc.vector.tensor_tensor(
+                z_bf[:].rearrange("p (c i t) -> p c t i", i=2, t=SLOTS),
+                first[:].rearrange("p t (c i) -> p c t i", i=2),
+                second[:].rearrange("p t (c i) -> p c t i", i=2),
+                ALU.max,
+            )
+            z_codes = sb("z_codes%d" % c, [P, nv], U32)
+            z_scales = sb("z_scales%d" % c, [P, nv], U8)
+            nc.vector.quantize_mx(out=z_codes[:].bitcast(X4), scales=z_scales[:], in_=z_bf[:])
+            for t in range(SLOTS):
+                cols = slice(t * P, (t + 1) * P)
+                nc.tensor.matmul_mx(
+                    out=h_acc[t][:, v0 : v0 + nv], lhsT=w2_codes[:, cols].bitcast(X4), lhsT_scale=w2_scales[:, cols],
+                    rhs=z_codes[:].bitcast(X4), rhs_scale=z_scales[:], start=True, stop=True,
+                )
+                nc.scalar.copy(h[t][:, v0 : v0 + nv], h_acc[t][:, v0 : v0 + nv])
+
+        w3_codes = sb("w3_codes", [P, N], U32)
+        w3_scales = sb("w3_scales", [P, N], U8)
+        w3_bf = sb("w3_bf", [P, N * SLOTS], BF16)
+        nc.scalar.copy(
+            w3_bf[:].rearrange("p (c i j) -> p c j i", i=RUN, j=SLOTS),
+            w3_raw[:].rearrange("p j (c i) -> p c j i", i=RUN),
+        )
+        nc.vector.quantize_mx(out=w3_codes[:].bitcast(X4), scales=w3_scales[:], in_=w3_bf[:])
+
+        z2 = [sb("z2_%d" % t, [P, V], F32) for t in range(SLOTS)]
+        z2_bf = [sb("z2_bf%d" % c, [P, OUT_CHUNK * SLOTS], BF16) for c in range(V // OUT_CHUNK)]
+        for g in range(2):
+            pa = sb("pa%d" % g, [P, 2, W], F32)
+            pb = sb("pb%d" % g, [P, 2, W], F32)
+            ra = sb("ra%d" % g, [P, 2, W], F32)
+            rb = sb("rb%d" % g, [P, 2, W], F32)
+            for u in range(2):
+                nc.vector.tensor_copy(pa[:, u, :], h[2 * g + u][:].indirect(n2_t[:]))
+                nc.vector.tensor_copy(pb[:, u, :], h[2 * g + u][:].indirect(n3_t[:]))
+            nc.vector.tensor_tensor(ra[:], pa[:], pb[:], ALU.max)
+            nc.vector.tensor_tensor(rb[:], pa[:], pb[:], ALU.min)
+            for u in range(2):
+                nc.vector.tensor_copy(z2[2 * g + u][:].indirect(n2_t[:]), ra[:, u, :])
+            for u in range(2):
+                t = 2 * g + u
+                nc.vector.tensor_copy(z2[t][:].indirect(n3_t[:]), rb[:, u, :])
+                for c in range(V // OUT_CHUNK):
+                    slots = z2_bf[c][:].rearrange("p (v t) -> p t v", t=SLOTS)
+                    nc.scalar.copy(slots[:, t], z2[t][:, c * OUT_CHUNK : (c + 1) * OUT_CHUNK])
+
+        out_rows = out.rearrange("(t p) v -> p t v", p=P)
+        for c in range(V // OUT_CHUNK):
+            vs = slice(c * OUT_CHUNK, (c + 1) * OUT_CHUNK)
+            z2_codes = sb("z2_codes%d" % c, [P, OUT_CHUNK], U32)
+            z2_scales = sb("z2_scales%d" % c, [P, OUT_CHUNK], U8)
+            nc.vector.quantize_mx(out=z2_codes[:].bitcast(X4), scales=z2_scales[:], in_=z2_bf[c][:])
+            acc = bank(c)
+            for t in range(N // P):
+                cols = slice(t * P, (t + 1) * P)
+                nc.tensor.matmul_mx(
+                    out=acc[:, cols], lhsT=w3_codes[:, cols].bitcast(X4), lhsT_scale=w3_scales[:, cols],
+                    rhs=z2_codes[:].bitcast(X4), rhs_scale=z2_scales[:], start=True, stop=True,
+                )
+            o = sb("o%d" % c, [P, N // P, OUT_CHUNK], F32)
+            nc.vector.tensor_tensor(o[:], acc[:].rearrange("p (t v) -> p t v", v=OUT_CHUNK), res_t[:, :, vs], ALU.add)
+            nc.sync.dma_start(out_rows[:, :, vs], o[:])

@@ -1,6 +1,7 @@
 from contextlib import ExitStack
 
 import concourse.mybir as mybir
+from concourse.masks import make_identity
 
 K, T, S, V, N, H, W = 512, 2048, 1024, 512, 512, 512, 256
 FLOPS = 2 * K * H * S + 2 * H * H * V + 2 * H * N * V
@@ -13,6 +14,7 @@ U16 = mybir.dt.uint16
 U8 = mybir.dt.uint8
 X4 = mybir.dt.float8_e4m3fn_x4
 ALU = mybir.AluOpType
+ACT = mybir.ActivationFunctionType
 
 P = 128
 SLOTS = 4
@@ -68,21 +70,36 @@ def tile_picked_deeppgaporder_none_p_kernel(tc, x_words, x_scales, w1, w2, w3, r
         nc.vector.tensor_copy(xs[:], xs_all[:].indirect(offs_t[:]))
         nc.vector.tensor_copy(xw[:], xw_all[:].bitcast(U32).indirect(offs_t[:]))
 
-        def deal_columns(copy, dst, raw, t):
+        def deal_columns(copy, dst, raw, t, runs=slice(0, P // RUN)):
             copy(
-                dst.rearrange("p (a q j) -> p a j q", q=RUN, j=SLOTS),
-                raw[:].rearrange("p j (a t q) -> p t a j q", t=SLOTS, q=RUN)[:, t],
+                dst.rearrange("p (a q j) -> p a j q", q=RUN, j=SLOTS)[:, runs],
+                raw[:].rearrange("p j (a t q) -> p t a j q", t=SLOTS, q=RUN)[:, t, runs],
             )
+
+        ident = sb("ident", [P, P], F32)
+        make_identity(nc, ident[:])
 
         w1_codes = sb("w1_codes", [P, H], U32)
         w1_scales = sb("w1_scales", [P, H], U8)
-        w1_bf = [sb("w1_bf%d" % t, [P, P * SLOTS], BF16) for t in range(SLOTS)]
         y = [sb("y%d" % t, [P, S], F32) for t in range(SLOTS)]
-        for t in range(SLOTS):
-            deal_columns(nc.scalar.copy if t < 2 else nc.vector.tensor_copy, w1_bf[t][:], w1_raw, t)
-        for t in range(SLOTS):
+
+        def quantize_w1(t, w_bf):
             cols = slice(t * P, (t + 1) * P)
-            nc.vector.quantize_mx(out=w1_codes[:, cols].bitcast(X4), scales=w1_scales[:, cols], in_=w1_bf[t][:])
+            nc.vector.quantize_mx(out=w1_codes[:, cols].bitcast(X4), scales=w1_scales[:, cols], in_=w_bf[:])
+
+        bf0 = sb("w1_even", [P, P * SLOTS], BF16)
+        bf1 = sb("w1_odd", [P, P * SLOTS], BF16)
+        deal_columns(nc.scalar.copy, bf0[:], w1_raw, 0, slice(0, 16))
+        deal_columns(nc.vector.tensor_copy, bf0[:], w1_raw, 0, slice(16, 32))
+        deal_columns(nc.scalar.copy, bf1[:], w1_raw, 1)
+        quantize_w1(0, bf0)
+        bf2 = sb("w1_even", [P, P * SLOTS], BF16)
+        deal_columns(nc.vector.tensor_copy, bf2[:], w1_raw, 2)
+        quantize_w1(1, bf1)
+        bf3 = sb("w1_odd", [P, P * SLOTS], BF16)
+        deal_columns(nc.vector.tensor_copy, bf3[:], w1_raw, 3)
+        quantize_w1(2, bf2)
+        quantize_w1(3, bf3)
         for t in range(SLOTS):
             cols = slice(t * P, (t + 1) * P)
             for half in range(S // BANK):
@@ -102,20 +119,77 @@ def tile_picked_deeppgaporder_none_p_kernel(tc, x_words, x_scales, w1, w2, w3, r
         nc.vector.quantize_mx(out=w2_codes[:].bitcast(X4), scales=w2_scales[:], in_=w2_bf[:])
 
         h = [sb("h%d" % t, [P, V], F32) for t in range(SLOTS)]
-        h_acc = [bank(4 + t) for t in range(SLOTS)]
-        for c, (v0, nv) in enumerate(Z_CHUNKS):
-            first = sb("first%d" % c, [P, SLOTS, nv], F32)
+
+        def line_up(name, v0, nv):
+            ln = sb(name, [P, SLOTS, 2 * nv], F32)
+            for t in range(SLOTS):
+                nc.vector.tensor_copy(ln[:, t, :], y[t][:].indirect(n1_t[:, v0 // 8 : (v0 + nv) // 8]))
+            return ln[:].rearrange("p t (v e) -> p e t v", e=2)
+
+        def multiply_w2(z_bf, v0, nv, accs, name):
+            z_codes = sb("z_codes" + name, [P, nv], U32)
+            z_scales = sb("z_scales" + name, [P, nv], U8)
+            nc.vector.quantize_mx(out=z_codes[:].bitcast(X4), scales=z_scales[:], in_=z_bf[:])
+            for t in range(SLOTS):
+                cols = slice(t * P, (t + 1) * P)
+                nc.tensor.matmul_mx(
+                    out=accs[t], lhsT=w2_codes[:, cols].bitcast(X4), lhsT_scale=w2_scales[:, cols],
+                    rhs=z_codes[:].bitcast(X4), rhs_scale=z_scales[:], start=True, stop=True,
+                )
+            for t in range(SLOTS):
+                nc.scalar.copy(h[t][:, v0 : v0 + nv], accs[t])
+
+        NA = 256
+        blocks = NA // P
+        zt_acc = [bank(4 + k) for k in range(blocks)]
+        diff = sb("diff", [P, SLOTS, NA], F32)
+        spread = sb("spread", [P, SLOTS, NA], F32)
+        pair = line_up("ln_a", 0, NA)
+        nc.vector.tensor_tensor(diff[:], pair[:, 0], pair[:, 1], ALU.subtract)
+        nc.scalar.activation(spread[:], diff[:], ACT.Abs, scale=3.0)
+        terms = [pair[:, 0], pair[:, 1], spread[:]]
+        for i, term in enumerate(terms):
+            for k in range(blocks):
+                for t in range(SLOTS):
+                    nc.tensor.matmul(
+                        zt_acc[k][:, t * P : (t + 1) * P], term[:, t, k * P : (k + 1) * P], ident[:],
+                        start=(i == 0 and t == 0), stop=(i == len(terms) - 1 and t == SLOTS - 1), is_transpose=True,
+                    )
+        zt_bf = sb("zt_bf", [P, blocks, BANK], BF16)
+        words_acc = bank(6)
+        for k in range(blocks):
+            nc.scalar.activation(
+                zt_bf[:, k, :].rearrange("v (u p e) -> v u p e", u=2, e=2),
+                zt_acc[k][:].rearrange("v (u e p) -> v u p e", u=2, e=2),
+                ACT.Copy, scale=0.25,
+            )
+            for u in range(2):
+                nc.tensor.transpose(
+                    words_acc[:, u * NA + k * P : u * NA + (k + 1) * P],
+                    zt_bf[:, k, :].bitcast(F32)[:, u * P : (u + 1) * P], ident[:],
+                )
+        za_bf = sb("za_bf", [P, NA * SLOTS], BF16)
+        nc.scalar.copy(
+            za_bf[:].bitcast(F32).rearrange("p (v u) -> p v u", u=2),
+            words_acc[:].rearrange("p (u v) -> p v u", u=2),
+        )
+        ha = [bank(k) for k in range(2)]
+        multiply_w2(za_bf, 0, NA, [ha[t // 2][:, (t % 2) * NA : (t % 2 + 1) * NA] for t in range(SLOTS)], "a")
+
+        w3_bf = sb("zt_bf", [P, N * SLOTS], BF16)
+        for k in range(SLOTS):
+            nc.scalar.copy(
+                w3_bf[:, k * BANK : (k + 1) * BANK].rearrange("p (c i j) -> p c j i", i=RUN, j=SLOTS),
+                w3_raw[:, :, k * P : (k + 1) * P].rearrange("p j (c i) -> p c j i", i=RUN),
+            )
+
+        for c in range(2):
+            v0, nv = NA + c * P, P
+            first = sb("za_bf" if c == 1 else "first", [P, SLOTS, nv], F32)
             second = sb("second%d" % c, [P, SLOTS, nv], F32)
-            lined = []
-            for t in range(SLOTS + 1):
-                if t < SLOTS:
-                    ln = sb("ln%d_%d" % (c, t), [P, 2 * nv], F32)
-                    nc.vector.tensor_copy(ln[:], y[t][:].indirect(n1_t[:, v0 // 8 : (v0 + nv) // 8]))
-                    lined.append(ln)
-                if t > 0:
-                    pair = lined[t - 1][:].rearrange("p (v e) -> p e v", e=2)
-                    nc.vector.scalar_tensor_tensor(first[:, t - 1, :], pair[:, 1], -0.5, pair[:, 0], ALU.mult, ALU.add)
-                    nc.vector.scalar_tensor_tensor(second[:, t - 1, :], pair[:, 0], -0.5, pair[:, 1], ALU.mult, ALU.add)
+            pair = line_up("ln_a" if c == 1 else "ln_b", v0, nv)
+            nc.vector.scalar_tensor_tensor(first[:], pair[:, 1], -0.5, pair[:, 0], ALU.mult, ALU.add)
+            nc.vector.scalar_tensor_tensor(second[:], pair[:, 0], -0.5, pair[:, 1], ALU.mult, ALU.add)
             z_bf = sb("z_bf%d" % c, [P, nv * SLOTS], BF16)
             nc.vector.tensor_tensor(
                 z_bf[:].rearrange("p (c i t) -> p c t i", i=2, t=SLOTS),
@@ -123,46 +197,38 @@ def tile_picked_deeppgaporder_none_p_kernel(tc, x_words, x_scales, w1, w2, w3, r
                 second[:].rearrange("p t (c i) -> p c t i", i=2),
                 ALU.max,
             )
-            z_codes = sb("z_codes%d" % c, [P, nv], U32)
-            z_scales = sb("z_scales%d" % c, [P, nv], U8)
-            nc.vector.quantize_mx(out=z_codes[:].bitcast(X4), scales=z_scales[:], in_=z_bf[:])
-            for t in range(SLOTS):
-                cols = slice(t * P, (t + 1) * P)
-                nc.tensor.matmul_mx(
-                    out=h_acc[t][:, v0 : v0 + nv], lhsT=w2_codes[:, cols].bitcast(X4), lhsT_scale=w2_scales[:, cols],
-                    rhs=z_codes[:].bitcast(X4), rhs_scale=z_scales[:], start=True, stop=True,
-                )
-                nc.scalar.copy(h[t][:, v0 : v0 + nv], h_acc[t][:, v0 : v0 + nv])
+            acc = bank(6 + c)
+            multiply_w2(z_bf, v0, nv, [acc[:, t * P : (t + 1) * P] for t in range(SLOTS)], "bc"[c])
 
-        w3_codes = sb("w3_codes", [P, N], U32)
+        w3_codes = sb("second1", [P, N], U32)
         w3_scales = sb("w3_scales", [P, N], U8)
-        w3_bf = sb("w3_bf", [P, N * SLOTS], BF16)
-        nc.scalar.copy(
-            w3_bf[:].rearrange("p (c i j) -> p c j i", i=RUN, j=SLOTS),
-            w3_raw[:].rearrange("p j (c i) -> p c j i", i=RUN),
-        )
         nc.vector.quantize_mx(out=w3_codes[:].bitcast(X4), scales=w3_scales[:], in_=w3_bf[:])
 
         z2 = [sb("z2_%d" % t, [P, V], F32) for t in range(SLOTS)]
         z2_bf = [sb("z2_bf%d" % c, [P, OUT_CHUNK * SLOTS], BF16) for c in range(V // OUT_CHUNK)]
-        for g in range(2):
-            pa = sb("pa%d" % g, [P, 2, W], F32)
-            pb = sb("pb%d" % g, [P, 2, W], F32)
-            ra = sb("ra%d" % g, [P, 2, W], F32)
-            rb = sb("rb%d" % g, [P, 2, W], F32)
-            for u in range(2):
-                nc.vector.tensor_copy(pa[:, u, :], h[2 * g + u][:].indirect(n2_t[:]))
-                nc.vector.tensor_copy(pb[:, u, :], h[2 * g + u][:].indirect(n3_t[:]))
-            nc.vector.tensor_tensor(ra[:], pa[:], pb[:], ALU.max)
-            nc.vector.tensor_tensor(rb[:], pa[:], pb[:], ALU.min)
-            for u in range(2):
-                nc.vector.tensor_copy(z2[2 * g + u][:].indirect(n2_t[:]), ra[:, u, :])
-            for u in range(2):
-                t = 2 * g + u
-                nc.vector.tensor_copy(z2[t][:].indirect(n3_t[:]), rb[:, u, :])
+        pb = [sb("pb%d" % t, [P, W], F32) for t in range(SLOTS)]
+        gap = [sb("gap%d" % t, [P, W], F32) for t in range(SLOTS)]
+        up = [sb("up%d" % t, [P, W], F32) for t in range(SLOTS)]
+        down = [sb("down%d" % t, [P, W], F32) for t in range(SLOTS)]
+        ndown = [sb("ndown%d" % t, [P, W], F32) for t in range(SLOTS)]
+        for t in range(SLOTS + 1):
+            if t < SLOTS:
+                nc.vector.tensor_copy(pb[t][:], h[t][:].indirect(n3_t[:]))
+            if t > 0:
+                g = t - 1
+                nc.vector.tensor_tensor(gap[g][:], h[g][:].indirect(n2_t[:]), pb[g][:], ALU.subtract)
+                nc.scalar.activation(up[g][:], gap[g][:], ACT.Relu)
+                nc.scalar.activation(ndown[g][:], gap[g][:], ACT.Relu, scale=-1.0)
+                nc.scalar.activation(down[g][:], ndown[g][:], ACT.Copy, scale=-1.0)
+        for t in range(SLOTS + 1):
+            if t < SLOTS:
+                nc.vector.tensor_tensor(z2[t][:].indirect(n2_t[:]), pb[t][:], up[t][:], ALU.add)
+            if t > 0:
+                g = t - 1
+                nc.vector.tensor_tensor(z2[g][:].indirect(n3_t[:]), pb[g][:], down[g][:], ALU.add)
                 for c in range(V // OUT_CHUNK):
                     slots = z2_bf[c][:].rearrange("p (v t) -> p t v", t=SLOTS)
-                    nc.scalar.copy(slots[:, t], z2[t][:, c * OUT_CHUNK : (c + 1) * OUT_CHUNK])
+                    nc.scalar.copy(slots[:, g], z2[g][:, c * OUT_CHUNK : (c + 1) * OUT_CHUNK])
 
         out_rows = out.rearrange("(t p) v -> p t v", p=P)
         for c in range(V // OUT_CHUNK):

@@ -46,9 +46,9 @@ def tile_picked_deeppgaporder_none_p_kernel(tc, x_words, x_scales, w1, w2, w3, r
         nc.sync.dma_start(offs_t[:], offs)
         for q in range(4):
             nc.sync.dma_start(xs_all[32 * q : 32 * q + 4, :].bitcast(I32), x_scales[0, 4 * q : 4 * q + 4, :].bitcast(I32))
-        nc.sync.dma_start(xw_all[:], x_words[0].rearrange("p c r -> p (c r)").bitcast(I32))
         w1_raw = sb("w1_raw", [P, SLOTS, H], F32)
         nc.sync.dma_start(w1_raw[:], w1.rearrange("(p j) h -> p j h", j=SLOTS))
+        nc.sync.dma_start(xw_all[:], x_words[0].rearrange("p c r -> p (c r)").bitcast(I32))
         nc.sync.dma_start(n1_t[:], n1)
 
         def load_dealt_rows(name, w):
@@ -68,12 +68,11 @@ def tile_picked_deeppgaporder_none_p_kernel(tc, x_words, x_scales, w1, w2, w3, r
         xs = sb("xs", [P, S], U8)
         xw = sb("xw", [P, S], U32)
         nc.vector.tensor_copy(xs[:], xs_all[:].indirect(offs_t[:]))
-        nc.vector.tensor_copy(xw[:], xw_all[:].bitcast(U32).indirect(offs_t[:]))
 
-        def deal_columns(copy, dst, raw, t, runs=slice(0, P // RUN)):
+        def deal_columns(copy, dst, raw, t):
             copy(
-                dst.rearrange("p (a q j) -> p a j q", q=RUN, j=SLOTS)[:, runs],
-                raw[:].rearrange("p j (a t q) -> p t a j q", t=SLOTS, q=RUN)[:, t, runs],
+                dst.rearrange("p (a q j) -> p a j q", q=RUN, j=SLOTS),
+                raw[:].rearrange("p j (a t q) -> p t a j q", t=SLOTS, q=RUN)[:, t],
             )
 
         ident = sb("ident", [P, P], F32)
@@ -83,126 +82,150 @@ def tile_picked_deeppgaporder_none_p_kernel(tc, x_words, x_scales, w1, w2, w3, r
         w1_scales = sb("w1_scales", [P, H], U8)
         y = [sb("y%d" % t, [P, S], F32) for t in range(SLOTS)]
 
-        def quantize_w1(t, w_bf):
-            cols = slice(t * P, (t + 1) * P)
-            nc.vector.quantize_mx(out=w1_codes[:, cols].bitcast(X4), scales=w1_scales[:, cols], in_=w_bf[:])
-
-        bf0 = sb("w1_even", [P, P * SLOTS], BF16)
-        bf1 = sb("w1_odd", [P, P * SLOTS], BF16)
-        deal_columns(nc.scalar.copy, bf0[:], w1_raw, 0, slice(0, 16))
-        deal_columns(nc.vector.tensor_copy, bf0[:], w1_raw, 0, slice(16, 32))
-        deal_columns(nc.scalar.copy, bf1[:], w1_raw, 1)
-        quantize_w1(0, bf0)
-        bf2 = sb("w1_even", [P, P * SLOTS], BF16)
-        deal_columns(nc.vector.tensor_copy, bf2[:], w1_raw, 2)
-        quantize_w1(1, bf1)
-        bf3 = sb("w1_odd", [P, P * SLOTS], BF16)
-        deal_columns(nc.vector.tensor_copy, bf3[:], w1_raw, 3)
-        quantize_w1(2, bf2)
-        quantize_w1(3, bf3)
+        w1_bf = [sb("w1_bf%d" % g, [P, 2 * BANK], BF16) for g in range(2)]
+        for t in range(SLOTS):
+            copy = nc.scalar.copy if t < 2 else nc.vector.tensor_copy
+            deal_columns(copy, w1_bf[t // 2][:, (t % 2) * BANK : (t % 2 + 1) * BANK], w1_raw, t)
+        for g in range(2):
+            cols = slice(g * 2 * P, (g + 1) * 2 * P)
+            nc.vector.quantize_mx(out=w1_codes[:, cols].bitcast(X4), scales=w1_scales[:, cols], in_=w1_bf[g][:])
+        pieces = [(0, 512), (512, 256), (768, 256)]
+        for s0, ns in pieces:
+            nc.vector.tensor_copy(xw[:, s0 : s0 + ns], xw_all[:].bitcast(U32).indirect(offs_t[:, s0 // 16 : (s0 + ns) // 16]))
+        turn = 0
         for t in range(SLOTS):
             cols = slice(t * P, (t + 1) * P)
-            for half in range(S // BANK):
-                tok = slice(half * BANK, (half + 1) * BANK)
-                acc = bank((2 * t + half) % 4)
+            for s0, ns in pieces if t == 0 else [(0, BANK), (BANK, BANK)]:
+                tok = slice(s0, s0 + ns)
+                acc = bank(turn % 4)
+                turn = turn + 1
                 nc.tensor.matmul_mx(
-                    out=acc[:], lhsT=w1_codes[:, cols].bitcast(X4), lhsT_scale=w1_scales[:, cols],
+                    out=acc[:, 0:ns], lhsT=w1_codes[:, cols].bitcast(X4), lhsT_scale=w1_scales[:, cols],
                     rhs=xw[:, tok].bitcast(X4), rhs_scale=xs[:, tok], start=True, stop=True,
                 )
-                nc.scalar.copy(y[t][:, tok], acc[:])
+                nc.scalar.copy(y[t][:, tok], acc[:, 0:ns])
 
-        w2_codes = sb("w2_codes", [P, H], U32)
         w2_scales = sb("w2_scales", [P, H], U8)
-        w2_bf = sb("w2_bf", [P, H * SLOTS], BF16)
+        w2_bf = sb("w1_codes", [P, H * SLOTS], BF16)
         for t in range(SLOTS):
             deal_columns(nc.scalar.copy, w2_bf[:, t * BANK : (t + 1) * BANK], w2_raw, t)
-        nc.vector.quantize_mx(out=w2_codes[:].bitcast(X4), scales=w2_scales[:], in_=w2_bf[:])
+
+        def interleave_w3(name, half):
+            w_bf = sb(name, [P, 2 * BANK], BF16)
+            for k in range(2):
+                c0 = (2 * half + k) * P
+                nc.scalar.copy(
+                    w_bf[:, k * BANK : (k + 1) * BANK].rearrange("p (c i j) -> p c j i", i=RUN, j=SLOTS),
+                    w3_raw[:, :, c0 : c0 + P].rearrange("p j (c i) -> p c j i", i=RUN),
+                )
+            return w_bf
+
+        w3_early = interleave_w3("w3_bf", 0)
 
         h = [sb("h%d" % t, [P, V], F32) for t in range(SLOTS)]
 
-        def line_up(name, v0, nv):
-            ln = sb(name, [P, SLOTS, 2 * nv], F32)
-            for t in range(SLOTS):
-                nc.vector.tensor_copy(ln[:, t, :], y[t][:].indirect(n1_t[:, v0 // 8 : (v0 + nv) // 8]))
-            return ln[:].rearrange("p t (v e) -> p e t v", e=2)
+        def line_up(ln, t, j0, nj):
+            nc.vector.tensor_copy(ln, y[t][:].indirect(n1_t[:, j0 // 16 : (j0 + nj) // 16]))
 
-        def multiply_w2(z_bf, v0, nv, accs, name):
+        def quantize(z_bf, nv, name):
             z_codes = sb("z_codes" + name, [P, nv], U32)
             z_scales = sb("z_scales" + name, [P, nv], U8)
-            nc.vector.quantize_mx(out=z_codes[:].bitcast(X4), scales=z_scales[:], in_=z_bf[:])
-            for t in range(SLOTS):
-                cols = slice(t * P, (t + 1) * P)
-                nc.tensor.matmul_mx(
-                    out=accs[t], lhsT=w2_codes[:, cols].bitcast(X4), lhsT_scale=w2_scales[:, cols],
-                    rhs=z_codes[:].bitcast(X4), rhs_scale=z_scales[:], start=True, stop=True,
-                )
-            for t in range(SLOTS):
-                nc.scalar.copy(h[t][:, v0 : v0 + nv], accs[t])
+            nc.vector.quantize_mx(out=z_codes[:].bitcast(X4), scales=z_scales[:], in_=z_bf)
+            return z_codes, z_scales
+
+        def multiply_w2(acc, t, z_mx):
+            cols = slice(t * P, (t + 1) * P)
+            nc.tensor.matmul_mx(
+                out=acc, lhsT=w2_codes[:, cols].bitcast(X4), lhsT_scale=w2_scales[:, cols],
+                rhs=z_mx[0][:].bitcast(X4), rhs_scale=z_mx[1][:], start=True, stop=True,
+            )
 
         NA = 256
         blocks = NA // P
         zt_acc = [bank(4 + k) for k in range(blocks)]
-        diff = sb("diff", [P, SLOTS, NA], F32)
-        spread = sb("spread", [P, SLOTS, NA], F32)
-        pair = line_up("ln_a", 0, NA)
-        nc.vector.tensor_tensor(diff[:], pair[:, 0], pair[:, 1], ALU.subtract)
-        nc.scalar.activation(spread[:], diff[:], ACT.Abs, scale=3.0)
-        terms = [pair[:, 0], pair[:, 1], spread[:]]
-        for i, term in enumerate(terms):
+
+        def add_turned(term, t, start, stop):
             for k in range(blocks):
-                for t in range(SLOTS):
-                    nc.tensor.matmul(
-                        zt_acc[k][:, t * P : (t + 1) * P], term[:, t, k * P : (k + 1) * P], ident[:],
-                        start=(i == 0 and t == 0), stop=(i == len(terms) - 1 and t == SLOTS - 1), is_transpose=True,
-                    )
+                nc.tensor.matmul(
+                    zt_acc[k][:, t * P : (t + 1) * P], term[:, k * P : (k + 1) * P], ident[:],
+                    start=start, stop=stop, is_transpose=True,
+                )
+
+        batches = [range(t, t + 1) for t in range(SLOTS)]
+        diffs = []
+        for b, slots in enumerate(batches):
+            ln = sb("ln%d" % b, [P, len(slots), 2 * NA], F32)
+            for i, t in enumerate(slots):
+                line_up(ln[:, i, :], t, 0, 2 * NA)
+            pair = ln[:].rearrange("p t (v e) -> p e t v", e=2)
+            diff = sb("diff%d" % b, [P, len(slots), NA], F32)
+            nc.gpsimd.tensor_tensor(diff[:], pair[:, 0], pair[:, 1], ALU.subtract)
+            diffs.append(diff)
+            for i, t in enumerate(slots):
+                add_turned(pair[:, 0, i], t, t == 0, False)
+                add_turned(pair[:, 1, i], t, False, False)
+        for b, slots in enumerate(batches):
+            spread = sb("spread%d" % b, [P, len(slots), NA], F32)
+            nc.scalar.activation(spread[:], diffs[b][:], ACT.Abs, scale=3.0)
+            for i, t in enumerate(slots):
+                add_turned(spread[:, i], t, False, t == SLOTS - 1)
+        w2_codes = sb("ln3", [P, H], U32)
+        nc.vector.quantize_mx(out=w2_codes[:].bitcast(X4), scales=w2_scales[:], in_=w2_bf[:])
         zt_bf = sb("zt_bf", [P, blocks, BANK], BF16)
-        words_acc = bank(6)
         for k in range(blocks):
             nc.scalar.activation(
                 zt_bf[:, k, :].rearrange("v (u p e) -> v u p e", u=2, e=2),
                 zt_acc[k][:].rearrange("v (u e p) -> v u p e", u=2, e=2),
                 ACT.Copy, scale=0.25,
             )
+        za_bf = sb("za_bf", [P, NA * SLOTS], BF16)
+        words_acc = bank(6)
+        for k in range(blocks):
             for u in range(2):
                 nc.tensor.transpose(
                     words_acc[:, u * NA + k * P : u * NA + (k + 1) * P],
                     zt_bf[:, k, :].bitcast(F32)[:, u * P : (u + 1) * P], ident[:],
                 )
-        za_bf = sb("za_bf", [P, NA * SLOTS], BF16)
         nc.scalar.copy(
             za_bf[:].bitcast(F32).rearrange("p (v u) -> p v u", u=2),
             words_acc[:].rearrange("p (u v) -> p v u", u=2),
         )
-        ha = [bank(k) for k in range(2)]
-        multiply_w2(za_bf, 0, NA, [ha[t // 2][:, (t % 2) * NA : (t % 2 + 1) * NA] for t in range(SLOTS)], "a")
+        za_mx = quantize(za_bf[:], NA, "a")
+        for t in range(SLOTS):
+            ha = bank(t)
+            multiply_w2(ha[:, 0:NA], t, za_mx)
+            nc.scalar.copy(h[t][:, 0:NA], ha[:, 0:NA])
+        w3_late = interleave_w3("zt_bf", 1)
 
-        w3_bf = sb("zt_bf", [P, N * SLOTS], BF16)
-        for k in range(SLOTS):
-            nc.scalar.copy(
-                w3_bf[:, k * BANK : (k + 1) * BANK].rearrange("p (c i j) -> p c j i", i=RUN, j=SLOTS),
-                w3_raw[:, :, k * P : (k + 1) * P].rearrange("p j (c i) -> p c j i", i=RUN),
-            )
-
-        for c in range(2):
-            v0, nv = NA + c * P, P
-            first = sb("za_bf" if c == 1 else "first", [P, SLOTS, nv], F32)
-            second = sb("second%d" % c, [P, SLOTS, nv], F32)
-            pair = line_up("ln_a" if c == 1 else "ln_b", v0, nv)
-            nc.vector.scalar_tensor_tensor(first[:], pair[:, 1], -0.5, pair[:, 0], ALU.mult, ALU.add)
-            nc.vector.scalar_tensor_tensor(second[:], pair[:, 0], -0.5, pair[:, 1], ALU.mult, ALU.add)
-            z_bf = sb("z_bf%d" % c, [P, nv * SLOTS], BF16)
+        nv = V - NA
+        first = sb("first", [P, SLOTS, nv], F32)
+        second = sb("second1", [P, SLOTS, nv], F32)
+        ln = sb("ln_rest", [P, SLOTS, 2 * nv], F32)
+        for t in range(SLOTS):
+            line_up(ln[:, t, :], t, 2 * NA, 2 * nv)
+        pair = ln[:].rearrange("p t (v e) -> p e t v", e=2)
+        nc.vector.scalar_tensor_tensor(first[:], pair[:, 1], -0.5, pair[:, 0], ALU.mult, ALU.add)
+        nc.vector.scalar_tensor_tensor(second[:], pair[:, 0], -0.5, pair[:, 1], ALU.mult, ALU.add)
+        z_bf = sb("za_bf", [P, nv * SLOTS], BF16)
+        for k in range(nv // P):
             nc.vector.tensor_tensor(
-                z_bf[:].rearrange("p (c i t) -> p c t i", i=2, t=SLOTS),
-                first[:].rearrange("p t (c i) -> p c t i", i=2),
-                second[:].rearrange("p t (c i) -> p c t i", i=2),
+                z_bf[:, k * BANK : (k + 1) * BANK].rearrange("p (c i t) -> p c t i", i=2, t=SLOTS),
+                first[:, :, k * P : (k + 1) * P].rearrange("p t (c i) -> p c t i", i=2),
+                second[:, :, k * P : (k + 1) * P].rearrange("p t (c i) -> p c t i", i=2),
                 ALU.max,
             )
-            acc = bank(6 + c)
-            multiply_w2(z_bf, v0, nv, [acc[:, t * P : (t + 1) * P] for t in range(SLOTS)], "bc"[c])
+        z_mx = [quantize(z_bf[:, k * BANK : (k + 1) * BANK], P, "bc"[k]) for k in range(nv // P)]
+        for t in range(SLOTS):
+            hc = bank(4 + t)
+            for k in range(nv // P):
+                multiply_w2(hc[:, k * P : (k + 1) * P], t, z_mx[k])
+            nc.scalar.copy(h[t][:, NA:V], hc[:, 0:nv])
 
         w3_codes = sb("second1", [P, N], U32)
         w3_scales = sb("w3_scales", [P, N], U8)
-        nc.vector.quantize_mx(out=w3_codes[:].bitcast(X4), scales=w3_scales[:], in_=w3_bf[:])
+        for half, w_bf in enumerate((w3_early, w3_late)):
+            cols = slice(half * 2 * P, (half + 1) * 2 * P)
+            nc.vector.quantize_mx(out=w3_codes[:, cols].bitcast(X4), scales=w3_scales[:, cols], in_=w_bf[:])
 
         z2 = [sb("z2_%d" % t, [P, V], F32) for t in range(SLOTS)]
         z2_bf = [sb("z2_bf%d" % c, [P, OUT_CHUNK * SLOTS], BF16) for c in range(V // OUT_CHUNK)]

@@ -19,12 +19,17 @@ ACT = mybir.ActivationFunctionType
 P = 128
 SLOTS = 4
 RUN = 4
+LIST_ROWS = 16
+QUADRANT = 32
 BANK = 512
-Z_CHUNKS = [(0, 256), (256, 128), (384, 128)]
-OUT_CHUNK = 128
+Y_BANKS = 4
+V_TENSOR = 256
+V_VECTOR = V - V_TENSOR
 
 
-def tile_picked_deeppgaporder_none_p_kernel(tc, x_words, x_scales, w1, w2, w3, res, offs, n1, n2, n3, out):
+def tile_picked_deeppgaporder_none_p_kernel(
+    tc, x_words, x_scales, w1, w2, w3, res, offs, n1, n2, n3, out
+):
     nc = tc.nc
     with ExitStack() as ctx:
         keep = ctx.enter_context(tc.tile_pool(name="keep", bufs=1))
@@ -36,38 +41,54 @@ def tile_picked_deeppgaporder_none_p_kernel(tc, x_words, x_scales, w1, w2, w3, r
         def bank(i):
             return psum.tile([P, BANK], F32, name="bank%d" % i)
 
-        offs_t = sb("offs_t", [P, S // 16], U16)
-        n1_t = sb("n1_t", [P, S // 16], U16)
-        n2_t = sb("n2_t", [P, W // 16], U16)
-        n3_t = sb("n3_t", [P, W // 16], U16)
+        def block(i):
+            return slice(i * P, (i + 1) * P)
+
+        def quantize(codes, scales, values):
+            nc.vector.quantize_mx(out=codes.bitcast(X4), scales=scales, in_=values)
+
+        def multiply(acc, w_codes, w_scales, codes, scales):
+            nc.tensor.matmul_mx(
+                out=acc, lhsT=w_codes.bitcast(X4), lhsT_scale=w_scales,
+                rhs=codes.bitcast(X4), rhs_scale=scales, start=True, stop=True,
+            )
+
+        offs_t = sb("offs_t", [P, S // LIST_ROWS], U16)
+        n1_t = sb("n1_t", [P, S // LIST_ROWS], U16)
+        n2_t = sb("n2_t", [P, W // LIST_ROWS], U16)
+        n3_t = sb("n3_t", [P, W // LIST_ROWS], U16)
         xs_all = sb("xs_all", [P, T], U8)
         xw_all = sb("xw_all", [P, T], I32)
-        nc.vector.memset(xs_all[:].bitcast(I32), 0)
         nc.sync.dma_start(offs_t[:], offs)
-        for q in range(4):
-            nc.sync.dma_start(xs_all[32 * q : 32 * q + 4, :].bitcast(I32), x_scales[0, 4 * q : 4 * q + 4, :].bitcast(I32))
+        for quad in range(P // QUADRANT):
+            rows = x_scales[0:1, 4 * quad : 4 * quad + 4, :].bitcast(I32)
+            nc.sync.dma_start(
+                xs_all[QUADRANT * quad : QUADRANT * (quad + 1), :].bitcast(I32),
+                rows.to_broadcast([QUADRANT // 4, 4, T // 4]),
+            )
+        nc.sync.dma_start(xw_all[:], x_words[0].rearrange("p c r -> p (c r)").bitcast(I32))
         w1_raw = sb("w1_raw", [P, SLOTS, H], F32)
         nc.sync.dma_start(w1_raw[:], w1.rearrange("(p j) h -> p j h", j=SLOTS))
-        nc.sync.dma_start(xw_all[:], x_words[0].rearrange("p c r -> p (c r)").bitcast(I32))
         nc.sync.dma_start(n1_t[:], n1)
 
-        def load_dealt_rows(name, w):
+        def load_feature_rows(name, w):
             raw = sb(name, [P, SLOTS, w.shape[1]], F32)
             rows = w.rearrange("(a t q) n -> t a q n", t=SLOTS, q=RUN)
             for t in range(SLOTS):
                 nc.sync.dma_start(raw[:, t, :], rows[t])
             return raw
 
-        w2_raw = load_dealt_rows("w2_raw", w2)
+        w2_raw = load_feature_rows("w2_raw", w2)
         nc.sync.dma_start(n2_t[:], n2)
         nc.sync.dma_start(n3_t[:], n3)
-        w3_raw = load_dealt_rows("w3_raw", w3)
+        w3_raw = load_feature_rows("w3_raw", w3)
         res_t = sb("res_t", [P, N // P, V], F32)
-        nc.sync.dma_start(res_t[:], res.rearrange("(t p) v -> p t v", p=P))
+        nc.sync.dma_start(res_t[:], res.rearrange("(m p) v -> p m v", p=P))
 
         xs = sb("xs", [P, S], U8)
         xw = sb("xw", [P, S], U32)
         nc.vector.tensor_copy(xs[:], xs_all[:].indirect(offs_t[:]))
+        nc.vector.tensor_copy(xw[:], xw_all[:].bitcast(U32).indirect(offs_t[:]))
 
         def deal_columns(copy, dst, raw, t):
             copy(
@@ -81,29 +102,21 @@ def tile_picked_deeppgaporder_none_p_kernel(tc, x_words, x_scales, w1, w2, w3, r
         w1_codes = sb("w1_codes", [P, H], U32)
         w1_scales = sb("w1_scales", [P, H], U8)
         y = [sb("y%d" % t, [P, S], F32) for t in range(SLOTS)]
-
-        w1_bf = [sb("w1_bf%d" % g, [P, 2 * BANK], BF16) for g in range(2)]
+        w1_bf = []
+        for t in range(2):
+            w1_bf.append(sb("w1_bf%d" % t, [P, BANK], BF16))
+            deal_columns(nc.scalar.copy, w1_bf[t][:], w1_raw, t)
         for t in range(SLOTS):
-            copy = nc.scalar.copy if t < 2 else nc.vector.tensor_copy
-            deal_columns(copy, w1_bf[t // 2][:, (t % 2) * BANK : (t % 2 + 1) * BANK], w1_raw, t)
-        for g in range(2):
-            cols = slice(g * 2 * P, (g + 1) * 2 * P)
-            nc.vector.quantize_mx(out=w1_codes[:, cols].bitcast(X4), scales=w1_scales[:, cols], in_=w1_bf[g][:])
-        pieces = [(0, 512), (512, 256), (768, 256)]
-        for s0, ns in pieces:
-            nc.vector.tensor_copy(xw[:, s0 : s0 + ns], xw_all[:].bitcast(U32).indirect(offs_t[:, s0 // 16 : (s0 + ns) // 16]))
-        turn = 0
+            quantize(w1_codes[:, block(t)], w1_scales[:, block(t)], w1_bf[t][:])
+            if t < 2:
+                w1_bf.append(sb("w1_bf%d" % t, [P, BANK], BF16))
+                deal_columns(nc.vector.tensor_copy, w1_bf[t + 2][:], w1_raw, t + 2)
         for t in range(SLOTS):
-            cols = slice(t * P, (t + 1) * P)
-            for s0, ns in pieces if t == 0 else [(0, BANK), (BANK, BANK)]:
-                tok = slice(s0, s0 + ns)
-                acc = bank(turn % 4)
-                turn = turn + 1
-                nc.tensor.matmul_mx(
-                    out=acc[:, 0:ns], lhsT=w1_codes[:, cols].bitcast(X4), lhsT_scale=w1_scales[:, cols],
-                    rhs=xw[:, tok].bitcast(X4), rhs_scale=xs[:, tok], start=True, stop=True,
-                )
-                nc.scalar.copy(y[t][:, tok], acc[:, 0:ns])
+            for half in range(S // BANK):
+                tok = slice(half * BANK, (half + 1) * BANK)
+                acc = bank((2 * t + half) % Y_BANKS)
+                multiply(acc[:], w1_codes[:, block(t)], w1_scales[:, block(t)], xw[:, tok], xs[:, tok])
+                nc.scalar.copy(y[t][:, tok], acc[:])
 
         w2_scales = sb("w2_scales", [P, H], U8)
         w2_bf = sb("w1_codes", [P, H * SLOTS], BF16)
@@ -113,10 +126,9 @@ def tile_picked_deeppgaporder_none_p_kernel(tc, x_words, x_scales, w1, w2, w3, r
         def interleave_w3(name, half):
             w_bf = sb(name, [P, 2 * BANK], BF16)
             for k in range(2):
-                c0 = (2 * half + k) * P
                 nc.scalar.copy(
                     w_bf[:, k * BANK : (k + 1) * BANK].rearrange("p (c i j) -> p c j i", i=RUN, j=SLOTS),
-                    w3_raw[:, :, c0 : c0 + P].rearrange("p j (c i) -> p c j i", i=RUN),
+                    w3_raw[:, :, block(2 * half + k)].rearrange("p j (c i) -> p c j i", i=RUN),
                 )
             return w_bf
 
@@ -124,53 +136,36 @@ def tile_picked_deeppgaporder_none_p_kernel(tc, x_words, x_scales, w1, w2, w3, r
 
         h = [sb("h%d" % t, [P, V], F32) for t in range(SLOTS)]
 
-        def line_up(ln, t, j0, nj):
-            nc.vector.tensor_copy(ln, y[t][:].indirect(n1_t[:, j0 // 16 : (j0 + nj) // 16]))
+        def line_up(dst, t, v0, nv):
+            entries = slice(2 * v0 // LIST_ROWS, 2 * (v0 + nv) // LIST_ROWS)
+            nc.vector.tensor_copy(dst, y[t][:].indirect(n1_t[:, entries]))
 
-        def quantize(z_bf, nv, name):
-            z_codes = sb("z_codes" + name, [P, nv], U32)
-            z_scales = sb("z_scales" + name, [P, nv], U8)
-            nc.vector.quantize_mx(out=z_codes[:].bitcast(X4), scales=z_scales[:], in_=z_bf)
-            return z_codes, z_scales
-
-        def multiply_w2(acc, t, z_mx):
-            cols = slice(t * P, (t + 1) * P)
-            nc.tensor.matmul_mx(
-                out=acc, lhsT=w2_codes[:, cols].bitcast(X4), lhsT_scale=w2_scales[:, cols],
-                rhs=z_mx[0][:].bitcast(X4), rhs_scale=z_mx[1][:], start=True, stop=True,
-            )
-
-        NA = 256
-        blocks = NA // P
-        zt_acc = [bank(4 + k) for k in range(blocks)]
+        blocks = V_TENSOR // P
+        zt_acc = [bank(Y_BANKS + k) for k in range(blocks)]
 
         def add_turned(term, t, start, stop):
             for k in range(blocks):
                 nc.tensor.matmul(
-                    zt_acc[k][:, t * P : (t + 1) * P], term[:, k * P : (k + 1) * P], ident[:],
-                    start=start, stop=stop, is_transpose=True,
+                    zt_acc[k][:, block(t)], term[:, block(k)], ident[:], start=start, stop=stop, is_transpose=True
                 )
 
-        batches = [range(t, t + 1) for t in range(SLOTS)]
         diffs = []
-        for b, slots in enumerate(batches):
-            ln = sb("ln%d" % b, [P, len(slots), 2 * NA], F32)
-            for i, t in enumerate(slots):
-                line_up(ln[:, i, :], t, 0, 2 * NA)
-            pair = ln[:].rearrange("p t (v e) -> p e t v", e=2)
-            diff = sb("diff%d" % b, [P, len(slots), NA], F32)
-            nc.gpsimd.tensor_tensor(diff[:], pair[:, 0], pair[:, 1], ALU.subtract)
-            diffs.append(diff)
-            for i, t in enumerate(slots):
-                add_turned(pair[:, 0, i], t, t == 0, False)
-                add_turned(pair[:, 1, i], t, False, False)
-        for b, slots in enumerate(batches):
-            spread = sb("spread%d" % b, [P, len(slots), NA], F32)
-            nc.scalar.activation(spread[:], diffs[b][:], ACT.Abs, scale=3.0)
-            for i, t in enumerate(slots):
-                add_turned(spread[:, i], t, False, t == SLOTS - 1)
-        w2_codes = sb("ln3", [P, H], U32)
-        nc.vector.quantize_mx(out=w2_codes[:].bitcast(X4), scales=w2_scales[:], in_=w2_bf[:])
+        for t in range(SLOTS):
+            lined = sb("lined%d" % t, [P, 2 * V_TENSOR], F32)
+            line_up(lined[:], t, 0, V_TENSOR)
+            pair = lined[:].rearrange("p (v e) -> p e v", e=2)
+            diffs.append(sb("diff%d" % t, [P, V_TENSOR], F32))
+            nc.gpsimd.tensor_tensor(diffs[t][:], pair[:, 0], pair[:, 1], ALU.subtract)
+            add_turned(pair[:, 0], t, t == 0, False)
+            add_turned(pair[:, 1], t, False, False)
+        for t in range(SLOTS):
+            spread = sb("spread%d" % t, [P, V_TENSOR], F32)
+            nc.scalar.activation(spread[:], diffs[t][:], ACT.Abs, scale=3.0)
+            add_turned(spread[:], t, False, t == SLOTS - 1)
+
+        w2_codes = sb("lined%d" % (SLOTS - 1), [P, H], U32)
+        quantize(w2_codes[:], w2_scales[:], w2_bf[:])
+
         zt_bf = sb("zt_bf", [P, blocks, BANK], BF16)
         for k in range(blocks):
             nc.scalar.activation(
@@ -178,94 +173,91 @@ def tile_picked_deeppgaporder_none_p_kernel(tc, x_words, x_scales, w1, w2, w3, r
                 zt_acc[k][:].rearrange("v (u e p) -> v u p e", u=2, e=2),
                 ACT.Copy, scale=0.25,
             )
-        za_bf = sb("za_bf", [P, NA * SLOTS], BF16)
-        words_acc = bank(6)
+        za_bf = sb("za_bf", [P, V_TENSOR * SLOTS], BF16)
+        pairs_acc = bank(Y_BANKS + blocks)
         for k in range(blocks):
             for u in range(2):
                 nc.tensor.transpose(
-                    words_acc[:, u * NA + k * P : u * NA + (k + 1) * P],
-                    zt_bf[:, k, :].bitcast(F32)[:, u * P : (u + 1) * P], ident[:],
+                    pairs_acc[:, block(u * blocks + k)], zt_bf[:, k, :].bitcast(F32)[:, block(u)], ident[:]
                 )
         nc.scalar.copy(
             za_bf[:].bitcast(F32).rearrange("p (v u) -> p v u", u=2),
-            words_acc[:].rearrange("p (u v) -> p v u", u=2),
+            pairs_acc[:].rearrange("p (u v) -> p v u", u=2),
         )
-        za_mx = quantize(za_bf[:], NA, "a")
-        for t in range(SLOTS):
-            ha = bank(t)
-            multiply_w2(ha[:, 0:NA], t, za_mx)
-            nc.scalar.copy(h[t][:, 0:NA], ha[:, 0:NA])
-        w3_late = interleave_w3("zt_bf", 1)
+        za_codes = sb("za_codes", [P, V_TENSOR], U32)
+        za_scales = sb("za_scales", [P, V_TENSOR], U8)
+        quantize(za_codes[:], za_scales[:], za_bf[:])
 
-        nv = V - NA
-        first = sb("first", [P, SLOTS, nv], F32)
-        second = sb("second1", [P, SLOTS, nv], F32)
-        ln = sb("ln_rest", [P, SLOTS, 2 * nv], F32)
+        a_less = sb("a_less", [P, SLOTS, V_VECTOR], F32)
+        b_less = sb("b_less", [P, SLOTS, V_VECTOR], F32)
+        lined = sb("lined_rest", [P, SLOTS, 2 * V_VECTOR], F32)
         for t in range(SLOTS):
-            line_up(ln[:, t, :], t, 2 * NA, 2 * nv)
-        pair = ln[:].rearrange("p t (v e) -> p e t v", e=2)
-        nc.vector.scalar_tensor_tensor(first[:], pair[:, 1], -0.5, pair[:, 0], ALU.mult, ALU.add)
-        nc.vector.scalar_tensor_tensor(second[:], pair[:, 0], -0.5, pair[:, 1], ALU.mult, ALU.add)
-        z_bf = sb("za_bf", [P, nv * SLOTS], BF16)
-        for k in range(nv // P):
+            line_up(lined[:, t, :], t, V_TENSOR, V_VECTOR)
+        pair = lined[:].rearrange("p t (v e) -> p e t v", e=2)
+        nc.vector.scalar_tensor_tensor(a_less[:], pair[:, 1], -0.5, pair[:, 0], ALU.mult, ALU.add)
+        nc.vector.scalar_tensor_tensor(b_less[:], pair[:, 0], -0.5, pair[:, 1], ALU.mult, ALU.add)
+        zv_bf = [sb(name, [P, BANK], BF16) for name in ("zb_bf", "za_bf")]
+        for k in range(V_VECTOR // P):
             nc.vector.tensor_tensor(
-                z_bf[:, k * BANK : (k + 1) * BANK].rearrange("p (c i t) -> p c t i", i=2, t=SLOTS),
-                first[:, :, k * P : (k + 1) * P].rearrange("p t (c i) -> p c t i", i=2),
-                second[:, :, k * P : (k + 1) * P].rearrange("p t (c i) -> p c t i", i=2),
+                zv_bf[k][:].rearrange("p (c i t) -> p c t i", i=2, t=SLOTS),
+                a_less[:, :, block(k)].rearrange("p t (c i) -> p c t i", i=2),
+                b_less[:, :, block(k)].rearrange("p t (c i) -> p c t i", i=2),
                 ALU.max,
             )
-        z_mx = [quantize(z_bf[:, k * BANK : (k + 1) * BANK], P, "bc"[k]) for k in range(nv // P)]
-        for t in range(SLOTS):
-            hc = bank(4 + t)
-            for k in range(nv // P):
-                multiply_w2(hc[:, k * P : (k + 1) * P], t, z_mx[k])
-            nc.scalar.copy(h[t][:, NA:V], hc[:, 0:nv])
+        zv_codes = [sb(name, [P, P], U32) for name in ("zt_bf", "zc_codes")]
+        zv_scales = [sb("zv_scales%d" % k, [P, P], U8) for k in range(V_VECTOR // P)]
+        for k in range(V_VECTOR // P):
+            quantize(zv_codes[k][:], zv_scales[k][:], zv_bf[k][:])
 
-        w3_codes = sb("second1", [P, N], U32)
+        for t in range(SLOTS):
+            acc = bank(t)
+            multiply(acc[:, 0:V_TENSOR], w2_codes[:, block(t)], w2_scales[:, block(t)], za_codes[:], za_scales[:])
+            nc.scalar.copy(h[t][:, 0:V_TENSOR], acc[:, 0:V_TENSOR])
+            acc = bank(SLOTS + t)
+            for k in range(V_VECTOR // P):
+                multiply(acc[:, block(k)], w2_codes[:, block(t)], w2_scales[:, block(t)], zv_codes[k][:], zv_scales[k][:])
+            nc.scalar.copy(h[t][:, V_TENSOR:V], acc[:, 0:V_VECTOR])
+
+        w3_late = interleave_w3("ident", 1)
+        w3_codes = sb("b_less", [P, N], U32)
         w3_scales = sb("w3_scales", [P, N], U8)
         for half, w_bf in enumerate((w3_early, w3_late)):
             cols = slice(half * 2 * P, (half + 1) * 2 * P)
-            nc.vector.quantize_mx(out=w3_codes[:, cols].bitcast(X4), scales=w3_scales[:, cols], in_=w_bf[:])
+            quantize(w3_codes[:, cols], w3_scales[:, cols], w_bf[:])
 
         z2 = [sb("z2_%d" % t, [P, V], F32) for t in range(SLOTS)]
-        z2_bf = [sb("z2_bf%d" % c, [P, OUT_CHUNK * SLOTS], BF16) for c in range(V // OUT_CHUNK)]
+        z2_bf = [sb("z2_bf%d" % c, [P, BANK], BF16) for c in range(V // P)]
         pb = [sb("pb%d" % t, [P, W], F32) for t in range(SLOTS)]
         gap = [sb("gap%d" % t, [P, W], F32) for t in range(SLOTS)]
-        up = [sb("up%d" % t, [P, W], F32) for t in range(SLOTS)]
-        down = [sb("down%d" % t, [P, W], F32) for t in range(SLOTS)]
-        ndown = [sb("ndown%d" % t, [P, W], F32) for t in range(SLOTS)]
-        for t in range(SLOTS + 1):
-            if t < SLOTS:
-                nc.vector.tensor_copy(pb[t][:], h[t][:].indirect(n3_t[:]))
-            if t > 0:
-                g = t - 1
-                nc.vector.tensor_tensor(gap[g][:], h[g][:].indirect(n2_t[:]), pb[g][:], ALU.subtract)
-                nc.scalar.activation(up[g][:], gap[g][:], ACT.Relu)
-                nc.scalar.activation(ndown[g][:], gap[g][:], ACT.Relu, scale=-1.0)
-                nc.scalar.activation(down[g][:], ndown[g][:], ACT.Copy, scale=-1.0)
-        for t in range(SLOTS + 1):
-            if t < SLOTS:
-                nc.vector.tensor_tensor(z2[t][:].indirect(n2_t[:]), pb[t][:], up[t][:], ALU.add)
-            if t > 0:
-                g = t - 1
-                nc.vector.tensor_tensor(z2[g][:].indirect(n3_t[:]), pb[g][:], down[g][:], ALU.add)
-                for c in range(V // OUT_CHUNK):
-                    slots = z2_bf[c][:].rearrange("p (v t) -> p t v", t=SLOTS)
-                    nc.scalar.copy(slots[:, g], z2[g][:, c * OUT_CHUNK : (c + 1) * OUT_CHUNK])
+        rise = [sb("rise%d" % t, [P, W], F32) for t in range(SLOTS)]
+        fall = [sb("fall%d" % t, [P, W], F32) for t in range(SLOTS)]
+        fall_size = [sb("fall_size%d" % t, [P, W], F32) for t in range(SLOTS)]
+        for step in range(SLOTS + 1):
+            if step < SLOTS:
+                nc.vector.tensor_copy(pb[step][:], h[step][:].indirect(n3_t[:]))
+            if step > 0:
+                t = step - 1
+                nc.vector.tensor_tensor(gap[t][:], h[t][:].indirect(n2_t[:]), pb[t][:], ALU.subtract)
+                nc.scalar.activation(rise[t][:], gap[t][:], ACT.Relu)
+                nc.scalar.activation(fall_size[t][:], gap[t][:], ACT.Relu, scale=-1.0)
+                nc.scalar.activation(fall[t][:], fall_size[t][:], ACT.Copy, scale=-1.0)
+        for step in range(SLOTS + 1):
+            if step < SLOTS:
+                nc.vector.tensor_tensor(z2[step][:].indirect(n2_t[:]), pb[step][:], rise[step][:], ALU.add)
+            if step > 0:
+                t = step - 1
+                nc.vector.tensor_tensor(z2[t][:].indirect(n3_t[:]), pb[t][:], fall[t][:], ALU.add)
+                for c in range(V // P):
+                    nc.scalar.copy(z2_bf[c][:].rearrange("p (v t) -> p t v", t=SLOTS)[:, t], z2[t][:, block(c)])
 
-        out_rows = out.rearrange("(t p) v -> p t v", p=P)
-        for c in range(V // OUT_CHUNK):
-            vs = slice(c * OUT_CHUNK, (c + 1) * OUT_CHUNK)
-            z2_codes = sb("z2_codes%d" % c, [P, OUT_CHUNK], U32)
-            z2_scales = sb("z2_scales%d" % c, [P, OUT_CHUNK], U8)
-            nc.vector.quantize_mx(out=z2_codes[:].bitcast(X4), scales=z2_scales[:], in_=z2_bf[c][:])
+        out_rows = out.rearrange("(m p) v -> p m v", p=P)
+        for c in range(V // P):
+            z2_codes = sb("z2_codes%d" % c, [P, P], U32)
+            z2_scales = sb("z2_scales%d" % c, [P, P], U8)
+            quantize(z2_codes[:], z2_scales[:], z2_bf[c][:])
             acc = bank(c)
-            for t in range(N // P):
-                cols = slice(t * P, (t + 1) * P)
-                nc.tensor.matmul_mx(
-                    out=acc[:, cols], lhsT=w3_codes[:, cols].bitcast(X4), lhsT_scale=w3_scales[:, cols],
-                    rhs=z2_codes[:].bitcast(X4), rhs_scale=z2_scales[:], start=True, stop=True,
-                )
-            o = sb("o%d" % c, [P, N // P, OUT_CHUNK], F32)
-            nc.vector.tensor_tensor(o[:], acc[:].rearrange("p (t v) -> p t v", v=OUT_CHUNK), res_t[:, :, vs], ALU.add)
-            nc.sync.dma_start(out_rows[:, :, vs], o[:])
+            for m in range(N // P):
+                multiply(acc[:, block(m)], w3_codes[:, block(m)], w3_scales[:, block(m)], z2_codes[:], z2_scales[:])
+            result = sb("result%d" % c, [P, N // P, P], F32)
+            nc.vector.tensor_tensor(result[:], acc[:].rearrange("p (m v) -> p m v", v=P), res_t[:, :, block(c)], ALU.add)
+            nc.sync.dma_start(out_rows[:, :, block(c)], result[:])

from contextlib import ExitStack

import concourse.mybir as mybir
from concourse.masks import make_identity

K, T, S, V, N, H, W = 512, 2048, 1024, 512, 512, 512, 256
FLOPS = 2 * K * H * S + 2 * H * H * V + 2 * H * N * V

F32 = mybir.dt.float32
BF16 = mybir.dt.bfloat16
I32 = mybir.dt.int32
U32 = mybir.dt.uint32
U16 = mybir.dt.uint16
U8 = mybir.dt.uint8
X4 = mybir.dt.float8_e4m3fn_x4
ALU = mybir.AluOpType
ACT = mybir.ActivationFunctionType

P = 128
SLOTS = 4
RUN = 4
LIST_ROWS = 16
QUADRANT = 32
BANK = 512
Y_BANKS = 4
V_TENSOR = 256
V_VECTOR = V - V_TENSOR


def tile_picked_deeppgaporder_none_p_kernel(
    tc, x_words, x_scales, w1, w2, w3, res, offs, n1, n2, n3, out
):
    nc = tc.nc
    with ExitStack() as ctx:
        keep = ctx.enter_context(tc.tile_pool(name="keep", bufs=1))
        psum = ctx.enter_context(tc.psum_pool(name="psum", bufs=1))

        def sb(name, shape, dtype):
            return keep.tile(shape, dtype, name=name, align_bytes=64)

        def bank(i):
            return psum.tile([P, BANK], F32, name="bank%d" % i)

        def block(i):
            return slice(i * P, (i + 1) * P)

        def quantize(codes, scales, values):
            nc.vector.quantize_mx(out=codes.bitcast(X4), scales=scales, in_=values)

        def multiply(acc, w_codes, w_scales, codes, scales):
            nc.tensor.matmul_mx(
                out=acc, lhsT=w_codes.bitcast(X4), lhsT_scale=w_scales,
                rhs=codes.bitcast(X4), rhs_scale=scales, start=True, stop=True,
            )

        offs_t = sb("offs_t", [P, S // LIST_ROWS], U16)
        n1_t = sb("n1_t", [P, S // LIST_ROWS], U16)
        n2_t = sb("n2_t", [P, W // LIST_ROWS], U16)
        n3_t = sb("n3_t", [P, W // LIST_ROWS], U16)
        xs_all = sb("xs_all", [P, T], U8)
        xw_all = sb("xw_all", [P, T], I32)
        nc.sync.dma_start(offs_t[:], offs)
        for quad in range(P // QUADRANT):
            rows = x_scales[0:1, 4 * quad : 4 * quad + 4, :].bitcast(I32)
            nc.sync.dma_start(
                xs_all[QUADRANT * quad : QUADRANT * (quad + 1), :].bitcast(I32),
                rows.to_broadcast([QUADRANT // 4, 4, T // 4]),
            )
        nc.sync.dma_start(xw_all[:], x_words[0].rearrange("p c r -> p (c r)").bitcast(I32))
        w1_raw = sb("w1_raw", [P, SLOTS, H], F32)
        nc.sync.dma_start(w1_raw[:], w1.rearrange("(p j) h -> p j h", j=SLOTS))
        nc.sync.dma_start(n1_t[:], n1)

        def load_feature_rows(name, w):
            raw = sb(name, [P, SLOTS, w.shape[1]], F32)
            rows = w.rearrange("(a t q) n -> t a q n", t=SLOTS, q=RUN)
            for t in range(SLOTS):
                nc.sync.dma_start(raw[:, t, :], rows[t])
            return raw

        w2_raw = load_feature_rows("w2_raw", w2)
        nc.sync.dma_start(n2_t[:], n2)
        nc.sync.dma_start(n3_t[:], n3)
        w3_raw = load_feature_rows("w3_raw", w3)
        res_t = sb("res_t", [P, N // P, V], F32)
        nc.sync.dma_start(res_t[:], res.rearrange("(m p) v -> p m v", p=P))

        xs = sb("xs", [P, S], U8)
        xw = sb("xw", [P, S], U32)
        nc.vector.tensor_copy(xs[:], xs_all[:].indirect(offs_t[:]))
        nc.vector.tensor_copy(xw[:], xw_all[:].bitcast(U32).indirect(offs_t[:]))

        def deal_columns(copy, dst, raw, t):
            copy(
                dst.rearrange("p (a q j) -> p a j q", q=RUN, j=SLOTS),
                raw[:].rearrange("p j (a t q) -> p t a j q", t=SLOTS, q=RUN)[:, t],
            )

        ident = sb("ident", [P, P], F32)
        make_identity(nc, ident[:])

        w1_codes = sb("w1_codes", [P, H], U32)
        w1_scales = sb("w1_scales", [P, H], U8)
        y = [sb("y%d" % t, [P, S], F32) for t in range(SLOTS)]
        w1_bf = []
        for t in range(2):
            w1_bf.append(sb("w1_bf%d" % t, [P, BANK], BF16))
            deal_columns(nc.scalar.copy, w1_bf[t][:], w1_raw, t)
        for t in range(SLOTS):
            quantize(w1_codes[:, block(t)], w1_scales[:, block(t)], w1_bf[t][:])
            if t < 2:
                w1_bf.append(sb("w1_bf%d" % t, [P, BANK], BF16))
                deal_columns(nc.vector.tensor_copy, w1_bf[t + 2][:], w1_raw, t + 2)
        for t in range(SLOTS):
            for half in range(S // BANK):
                tok = slice(half * BANK, (half + 1) * BANK)
                acc = bank((2 * t + half) % Y_BANKS)
                multiply(acc[:], w1_codes[:, block(t)], w1_scales[:, block(t)], xw[:, tok], xs[:, tok])
                nc.scalar.copy(y[t][:, tok], acc[:])

        w2_scales = sb("w2_scales", [P, H], U8)
        w2_bf = sb("w1_codes", [P, H * SLOTS], BF16)
        for t in range(SLOTS):
            deal_columns(nc.scalar.copy, w2_bf[:, t * BANK : (t + 1) * BANK], w2_raw, t)

        def interleave_w3(name, half):
            w_bf = sb(name, [P, 2 * BANK], BF16)
            for k in range(2):
                nc.scalar.copy(
                    w_bf[:, k * BANK : (k + 1) * BANK].rearrange("p (c i j) -> p c j i", i=RUN, j=SLOTS),
                    w3_raw[:, :, block(2 * half + k)].rearrange("p j (c i) -> p c j i", i=RUN),
                )
            return w_bf

        w3_early = interleave_w3("w3_bf", 0)

        h = [sb("h%d" % t, [P, V], F32) for t in range(SLOTS)]

        def line_up(dst, t, v0, nv):
            entries = slice(2 * v0 // LIST_ROWS, 2 * (v0 + nv) // LIST_ROWS)
            nc.vector.tensor_copy(dst, y[t][:].indirect(n1_t[:, entries]))

        blocks = V_TENSOR // P
        zt_acc = [bank(Y_BANKS + k) for k in range(blocks)]

        def add_turned(term, t, start, stop):
            for k in range(blocks):
                nc.tensor.matmul(
                    zt_acc[k][:, block(t)], term[:, block(k)], ident[:], start=start, stop=stop, is_transpose=True
                )

        diffs = []
        for t in range(SLOTS):
            lined = sb("lined%d" % t, [P, 2 * V_TENSOR], F32)
            line_up(lined[:], t, 0, V_TENSOR)
            pair = lined[:].rearrange("p (v e) -> p e v", e=2)
            diffs.append(sb("diff%d" % t, [P, V_TENSOR], F32))
            nc.gpsimd.tensor_tensor(diffs[t][:], pair[:, 0], pair[:, 1], ALU.subtract)
            add_turned(pair[:, 0], t, t == 0, False)
            add_turned(pair[:, 1], t, False, False)
        for t in range(SLOTS):
            spread = sb("spread%d" % t, [P, V_TENSOR], F32)
            nc.scalar.activation(spread[:], diffs[t][:], ACT.Abs, scale=3.0)
            add_turned(spread[:], t, False, t == SLOTS - 1)

        w2_codes = sb("lined%d" % (SLOTS - 1), [P, H], U32)
        quantize(w2_codes[:], w2_scales[:], w2_bf[:])

        zt_bf = sb("zt_bf", [P, blocks, BANK], BF16)
        for k in range(blocks):
            nc.scalar.activation(
                zt_bf[:, k, :].rearrange("v (u p e) -> v u p e", u=2, e=2),
                zt_acc[k][:].rearrange("v (u e p) -> v u p e", u=2, e=2),
                ACT.Copy, scale=0.25,
            )
        za_bf = sb("za_bf", [P, V_TENSOR * SLOTS], BF16)
        pairs_acc = bank(Y_BANKS + blocks)
        for k in range(blocks):
            for u in range(2):
                nc.tensor.transpose(
                    pairs_acc[:, block(u * blocks + k)], zt_bf[:, k, :].bitcast(F32)[:, block(u)], ident[:]
                )
        nc.scalar.copy(
            za_bf[:].bitcast(F32).rearrange("p (v u) -> p v u", u=2),
            pairs_acc[:].rearrange("p (u v) -> p v u", u=2),
        )
        za_codes = sb("za_codes", [P, V_TENSOR], U32)
        za_scales = sb("za_scales", [P, V_TENSOR], U8)
        quantize(za_codes[:], za_scales[:], za_bf[:])

        a_less = sb("a_less", [P, SLOTS, V_VECTOR], F32)
        b_less = sb("b_less", [P, SLOTS, V_VECTOR], F32)
        lined = sb("lined_rest", [P, SLOTS, 2 * V_VECTOR], F32)
        for t in range(SLOTS):
            line_up(lined[:, t, :], t, V_TENSOR, V_VECTOR)
        pair = lined[:].rearrange("p t (v e) -> p e t v", e=2)
        nc.vector.scalar_tensor_tensor(a_less[:], pair[:, 1], -0.5, pair[:, 0], ALU.mult, ALU.add)
        nc.vector.scalar_tensor_tensor(b_less[:], pair[:, 0], -0.5, pair[:, 1], ALU.mult, ALU.add)
        zv_bf = [sb(name, [P, BANK], BF16) for name in ("zb_bf", "za_bf")]
        for k in range(V_VECTOR // P):
            nc.vector.tensor_tensor(
                zv_bf[k][:].rearrange("p (c i t) -> p c t i", i=2, t=SLOTS),
                a_less[:, :, block(k)].rearrange("p t (c i) -> p c t i", i=2),
                b_less[:, :, block(k)].rearrange("p t (c i) -> p c t i", i=2),
                ALU.max,
            )
        zv_codes = [sb(name, [P, P], U32) for name in ("zt_bf", "zc_codes")]
        zv_scales = [sb("zv_scales%d" % k, [P, P], U8) for k in range(V_VECTOR // P)]
        for k in range(V_VECTOR // P):
            quantize(zv_codes[k][:], zv_scales[k][:], zv_bf[k][:])

        for t in range(SLOTS):
            acc = bank(t)
            multiply(acc[:, 0:V_TENSOR], w2_codes[:, block(t)], w2_scales[:, block(t)], za_codes[:], za_scales[:])
            nc.scalar.copy(h[t][:, 0:V_TENSOR], acc[:, 0:V_TENSOR])
            acc = bank(SLOTS + t)
            for k in range(V_VECTOR // P):
                multiply(acc[:, block(k)], w2_codes[:, block(t)], w2_scales[:, block(t)], zv_codes[k][:], zv_scales[k][:])
            nc.scalar.copy(h[t][:, V_TENSOR:V], acc[:, 0:V_VECTOR])

        w3_late = interleave_w3("ident", 1)
        w3_codes = sb("b_less", [P, N], U32)
        w3_scales = sb("w3_scales", [P, N], U8)
        for half, w_bf in enumerate((w3_early, w3_late)):
            cols = slice(half * 2 * P, (half + 1) * 2 * P)
            quantize(w3_codes[:, cols], w3_scales[:, cols], w_bf[:])

        z2 = [sb("z2_%d" % t, [P, V], F32) for t in range(SLOTS)]
        z2_bf = [sb("z2_bf%d" % c, [P, BANK], BF16) for c in range(V // P)]
        pb = [sb("pb%d" % t, [P, W], F32) for t in range(SLOTS)]
        gap = [sb("gap%d" % t, [P, W], F32) for t in range(SLOTS)]
        rise = [sb("rise%d" % t, [P, W], F32) for t in range(SLOTS)]
        fall = [sb("fall%d" % t, [P, W], F32) for t in range(SLOTS)]
        fall_size = [sb("fall_size%d" % t, [P, W], F32) for t in range(SLOTS)]
        for step in range(SLOTS + 1):
            if step < SLOTS:
                nc.vector.tensor_copy(pb[step][:], h[step][:].indirect(n3_t[:]))
            if step > 0:
                t = step - 1
                nc.vector.tensor_tensor(gap[t][:], h[t][:].indirect(n2_t[:]), pb[t][:], ALU.subtract)
                nc.scalar.activation(rise[t][:], gap[t][:], ACT.Relu)
                nc.scalar.activation(fall_size[t][:], gap[t][:], ACT.Relu, scale=-1.0)
                nc.scalar.activation(fall[t][:], fall_size[t][:], ACT.Copy, scale=-1.0)
        for step in range(SLOTS + 1):
            if step < SLOTS:
                nc.vector.tensor_tensor(z2[step][:].indirect(n2_t[:]), pb[step][:], rise[step][:], ALU.add)
            if step > 0:
                t = step - 1
                nc.vector.tensor_tensor(z2[t][:].indirect(n3_t[:]), pb[t][:], fall[t][:], ALU.add)
                for c in range(V // P):
                    nc.scalar.copy(z2_bf[c][:].rearrange("p (v t) -> p t v", t=SLOTS)[:, t], z2[t][:, block(c)])

        out_rows = out.rearrange("(m p) v -> p m v", p=P)
        for c in range(V // P):
            z2_codes = sb("z2_codes%d" % c, [P, P], U32)
            z2_scales = sb("z2_scales%d" % c, [P, P], U8)
            quantize(z2_codes[:], z2_scales[:], z2_bf[c][:])
            acc = bank(c)
            for m in range(N // P):
                multiply(acc[:, block(m)], w3_codes[:, block(m)], w3_scales[:, block(m)], z2_codes[:], z2_scales[:])
            result = sb("result%d" % c, [P, N // P, P], F32)
            nc.vector.tensor_tensor(result[:], acc[:].rearrange("p (m v) -> p m v", v=P), res_t[:, :, block(c)], ALU.add)
            nc.sync.dma_start(out_rows[:, :, block(c)], result[:])
